import numpy as np
import ml_dtypes

BF16 = ml_dtypes.bfloat16


def bf(x):
    return np.asarray(x, np.float32).astype(BF16)


def f32(x):
    return np.asarray(x, np.float32)


def f64(x):
    return np.asarray(x).astype(np.float64)


def striped(idx):
    return np.tile(idx.reshape(-1, 16).T, (8, 1))


S, K, M, N, E, Q = 1024, 128, 128, 2048, 8, 256


def gelu_tanh(v):
    return 0.5 * v * (1.0 + np.tanh(np.sqrt(2.0 / np.pi) * (v + 0.044715 * v**3)))


def two_experts():
    first = np.random.permutation(S).reshape(E, S // E)
    return np.concatenate([np.random.permutation(np.concatenate([first[e], first[(e + 1) % E]])) for e in range(E)])


def setup_inputs():
    return {"table": bf(np.random.standard_normal((K, S))), "w": bf(np.random.standard_normal((E, K, M)) / np.sqrt(K)), "b": f32(0.5 * np.random.standard_normal((M, 1))), "offs": striped(two_experts())}


def reference(table, w, b, offs):
    idx = offs[:16].T.reshape(-1)
    x = f64(table)[:, idx]
    y = np.concatenate([f64(w)[e].T @ x[:, e * Q : (e + 1) * Q] for e in range(E)], axis=1)
    return gelu_tanh(y + f64(b))

@@ -1,0 +1,44 @@
+import concourse.mybir as mybir
+
+BF16, F32, U16 = mybir.dt.bfloat16, mybir.dt.float32, mybir.dt.uint16
+GELU_TANH = mybir.ActivationFunctionType.Gelu_apprx_tanh
+
+FEATURES = 128
+HIDDEN = 128
+TOKENS = 1024
+EXPERTS = 8
+PIECE = 256
+ENTRIES = EXPERTS * PIECE
+PER_COLUMN = 16
+
+FLOPS = 2 * FEATURES * HIDDEN * ENTRIES
+
+
+def tile_gather_matmul_kernel(tc, table, w, b, offs, out):
+    nc = tc.nc
+    with (
+        tc.tile_pool(name="held", bufs=1) as held,
+        tc.psum_pool(name="banks", bufs=1) as banks,
+    ):
+        offsets = held.tile([FEATURES, ENTRIES // PER_COLUMN], U16, name="offsets")
+        nc.sync.dma_start(offsets[:], offs)
+
+        tokens = held.tile([FEATURES, TOKENS], BF16, name="tokens")
+        nc.scalar.dma_start(tokens[:], table)
+
+        weights = held.tile([FEATURES, EXPERTS, HIDDEN], BF16, name="weights")
+        nc.sync.dma_start(weights[:], w.rearrange("e k m -> k e m"))
+
+        bias = held.tile([HIDDEN, 1], F32, name="bias")
+        nc.scalar.dma_start(bias[:], b)
+
+        result = held.tile([HIDDEN, ENTRIES], F32, name="result")
+
+        for e in range(EXPERTS):
+            columns = slice(e * PIECE, (e + 1) * PIECE)
+            piece = offsets[:, e * PIECE // PER_COLUMN : (e + 1) * PIECE // PER_COLUMN]
+
+            bank = banks.tile([HIDDEN, PIECE], F32, name="bank%d" % e)
+            nc.tensor.matmul(bank[:], weights[:, e, :], tokens[:].indirect(piece), start=True, stop=True)
+            nc.scalar.activation(result[:, columns], bank[:], GELU_TANH, bias=bias[:, 0:1])
+            nc.sync.dma_start(out[:, columns], result[:, columns])

@@ -32,6 +32,11 @@ def tile_gather_matmul_kernel(tc, table, w, b, offs, out):
         bias = held.tile([HIDDEN, 1], F32, name="bias")
         nc.scalar.dma_start(bias[:], b)
 
+        zeros = held.tile([HIDDEN, 1], F32, name="zeros")
+        nc.vector.memset(zeros[:], 0.0)
+        warmed = held.tile([HIDDEN, 1], F32, name="warmed")
+        nc.scalar.activation(warmed[:], zeros[:], GELU_TANH)
+
         result = held.tile([HIDDEN, ENTRIES], F32, name="result")
 
         for e in range(EXPERTS):

@@ -24,10 +24,11 @@ def tile_gather_matmul_kernel(tc, table, w, b, offs, out):
         nc.sync.dma_start(offsets[:], offs)
 
         tokens = held.tile([FEATURES, TOKENS], BF16, name="tokens")
-        nc.scalar.dma_start(tokens[:], table)
+        nc.sync.dma_start(tokens[:], table)
 
         weights = held.tile([FEATURES, EXPERTS, HIDDEN], BF16, name="weights")
-        nc.sync.dma_start(weights[:], w.rearrange("e k m -> k e m"))
+        for e in range(0, EXPERTS, 2):
+            nc.sync.dma_start(weights[:, e : e + 2, :], w[e : e + 2].rearrange("e k m -> k e m"))
 
         bias = held.tile([HIDDEN, 1], F32, name="bias")
         nc.scalar.dma_start(bias[:], b)

@@ -11,6 +11,9 @@ PIECE = 256
 ENTRIES = EXPERTS * PIECE
 PER_COLUMN = 16
 
+EXPERT_BANKS = 7
+WARM_MATMULS = 9
+
 FLOPS = 2 * FEATURES * HIDDEN * ENTRIES
 
 
@@ -18,7 +21,8 @@ def tile_gather_matmul_kernel(tc, table, w, b, offs, out):
     nc = tc.nc
     with (
         tc.tile_pool(name="held", bufs=1) as held,
-        tc.psum_pool(name="banks", bufs=1) as banks,
+        tc.psum_pool(name="banks", bufs=EXPERT_BANKS) as banks,
+        tc.psum_pool(name="spare", bufs=1) as spare,
     ):
         offsets = held.tile([FEATURES, ENTRIES // PER_COLUMN], U16, name="offsets")
         nc.sync.dma_start(offsets[:], offs)
@@ -33,10 +37,14 @@ def tile_gather_matmul_kernel(tc, table, w, b, offs, out):
         bias = held.tile([HIDDEN, 1], F32, name="bias")
         nc.scalar.dma_start(bias[:], b)
 
-        zeros = held.tile([HIDDEN, 1], F32, name="zeros")
+        zeros = held.tile([FEATURES, PIECE], BF16, name="zeros")
         nc.vector.memset(zeros[:], 0.0)
         warmed = held.tile([HIDDEN, 1], F32, name="warmed")
-        nc.scalar.activation(warmed[:], zeros[:], GELU_TANH)
+        nc.scalar.activation(warmed[:], zeros[:, 0:1], GELU_TANH)
+
+        unread = spare.tile([HIDDEN, PIECE], F32, name="unread")
+        for i in range(WARM_MATMULS):
+            nc.tensor.matmul(unread[:], zeros[:, 0:HIDDEN], zeros[:], start=True, stop=True)
 
         result = held.tile([HIDDEN, ENTRIES], F32, name="result")
 
@@ -44,7 +52,7 @@ def tile_gather_matmul_kernel(tc, table, w, b, offs, out):
             columns = slice(e * PIECE, (e + 1) * PIECE)
             piece = offsets[:, e * PIECE // PER_COLUMN : (e + 1) * PIECE // PER_COLUMN]
 
-            bank = banks.tile([HIDDEN, PIECE], F32, name="bank%d" % e)
+            bank = banks.tile([HIDDEN, PIECE], F32, name="bank")
             nc.tensor.matmul(bank[:], weights[:, e, :], tokens[:].indirect(piece), start=True, stop=True)
             nc.scalar.activation(result[:, columns], bank[:], GELU_TANH, bias=bias[:, 0:1])
             nc.sync.dma_start(out[:, columns], result[:, columns])

@@ -11,9 +11,6 @@ PIECE = 256
 ENTRIES = EXPERTS * PIECE
 PER_COLUMN = 16
 
-EXPERT_BANKS = 7
-WARM_MATMULS = 9
-
 FLOPS = 2 * FEATURES * HIDDEN * ENTRIES
 
 
@@ -21,14 +18,13 @@ def tile_gather_matmul_kernel(tc, table, w, b, offs, out):
     nc = tc.nc
     with (
         tc.tile_pool(name="held", bufs=1) as held,
-        tc.psum_pool(name="banks", bufs=EXPERT_BANKS) as banks,
-        tc.psum_pool(name="spare", bufs=1) as spare,
+        tc.psum_pool(name="banks", bufs=1) as banks,
     ):
         offsets = held.tile([FEATURES, ENTRIES // PER_COLUMN], U16, name="offsets")
         nc.sync.dma_start(offsets[:], offs)
 
         tokens = held.tile([FEATURES, TOKENS], BF16, name="tokens")
-        nc.sync.dma_start(tokens[:], table)
+        nc.scalar.dma_start(tokens[:], table)
 
         weights = held.tile([FEATURES, EXPERTS, HIDDEN], BF16, name="weights")
         for e in range(0, EXPERTS, 2):
@@ -37,14 +33,10 @@ def tile_gather_matmul_kernel(tc, table, w, b, offs, out):
         bias = held.tile([HIDDEN, 1], F32, name="bias")
         nc.scalar.dma_start(bias[:], b)
 
-        zeros = held.tile([FEATURES, PIECE], BF16, name="zeros")
+        zeros = held.tile([HIDDEN, 1], F32, name="zeros")
         nc.vector.memset(zeros[:], 0.0)
         warmed = held.tile([HIDDEN, 1], F32, name="warmed")
-        nc.scalar.activation(warmed[:], zeros[:, 0:1], GELU_TANH)
-
-        unread = spare.tile([HIDDEN, PIECE], F32, name="unread")
-        for i in range(WARM_MATMULS):
-            nc.tensor.matmul(unread[:], zeros[:, 0:HIDDEN], zeros[:], start=True, stop=True)
+        nc.scalar.activation(warmed[:], zeros[:], GELU_TANH)
 
         result = held.tile([HIDDEN, ENTRIES], F32, name="result")
 
@@ -52,7 +44,7 @@ def tile_gather_matmul_kernel(tc, table, w, b, offs, out):
             columns = slice(e * PIECE, (e + 1) * PIECE)
             piece = offsets[:, e * PIECE // PER_COLUMN : (e + 1) * PIECE // PER_COLUMN]
 
-            bank = banks.tile([HIDDEN, PIECE], F32, name="bank")
+            bank = banks.tile([HIDDEN, PIECE], F32, name="bank%d" % e)
             nc.tensor.matmul(bank[:], weights[:, e, :], tokens[:].indirect(piece), start=True, stop=True)
             nc.scalar.activation(result[:, columns], bank[:], GELU_TANH, bias=bias[:, 0:1])
             nc.sync.dma_start(out[:, columns], result[:, columns])

@@ -27,11 +27,13 @@ def tile_gather_matmul_kernel(tc, table, w, b, offs, out):
         nc.scalar.dma_start(tokens[:], table)
 
         weights = held.tile([FEATURES, EXPERTS, HIDDEN], BF16, name="weights")
-        for e in range(0, EXPERTS, 2):
-            nc.sync.dma_start(weights[:, e : e + 2, :], w[e : e + 2].rearrange("e k m -> k e m"))
+        nc.sync.dma_start(weights[:, 0:2, :], w[0:2].rearrange("e k m -> k e m"))
 
         bias = held.tile([HIDDEN, 1], F32, name="bias")
         nc.scalar.dma_start(bias[:], b)
+
+        for e in range(2, EXPERTS, 2):
+            nc.scalar.dma_start(weights[:, e : e + 2, :], w[e : e + 2].rearrange("e k m -> k e m"))
 
         zeros = held.tile([HIDDEN, 1], F32, name="zeros")
         nc.vector.memset(zeros[:], 0.0)

@@ -30,7 +30,7 @@ def tile_gather_matmul_kernel(tc, table, w, b, offs, out):
         nc.sync.dma_start(weights[:, 0:2, :], w[0:2].rearrange("e k m -> k e m"))
 
         bias = held.tile([HIDDEN, 1], F32, name="bias")
-        nc.scalar.dma_start(bias[:], b)
+        nc.sync.dma_start(bias[:], b)
 
         for e in range(2, EXPERTS, 2):
             nc.scalar.dma_start(weights[:, e : e + 2, :], w[e : e + 2].rearrange("e k m -> k e m"))

@@ -27,13 +27,13 @@ def tile_gather_matmul_kernel(tc, table, w, b, offs, out):
         nc.scalar.dma_start(tokens[:], table)
 
         weights = held.tile([FEATURES, EXPERTS, HIDDEN], BF16, name="weights")
-        nc.sync.dma_start(weights[:, 0:2, :], w[0:2].rearrange("e k m -> k e m"))
+        nc.sync.dma_start(weights[:, 0:1, :], w[0:1].rearrange("e k m -> k e m"))
 
         bias = held.tile([HIDDEN, 1], F32, name="bias")
         nc.sync.dma_start(bias[:], b)
 
-        for e in range(2, EXPERTS, 2):
-            nc.scalar.dma_start(weights[:, e : e + 2, :], w[e : e + 2].rearrange("e k m -> k e m"))
+        for group in (slice(1, 2), slice(2, 4), slice(4, 6), slice(6, 8)):
+            nc.scalar.dma_start(weights[:, group, :], w[group].rearrange("e k m -> k e m"))
 
         zeros = held.tile([HIDDEN, 1], F32, name="zeros")
         nc.vector.memset(zeros[:], 0.0)

@@ -10,6 +10,7 @@ EXPERTS = 8
 PIECE = 256
 ENTRIES = EXPERTS * PIECE
 PER_COLUMN = 16
+DMA_BLOCK = 256
 
 FLOPS = 2 * FEATURES * HIDDEN * ENTRIES
 
@@ -20,13 +21,14 @@ def tile_gather_matmul_kernel(tc, table, w, b, offs, out):
         tc.tile_pool(name="held", bufs=1) as held,
         tc.psum_pool(name="banks", bufs=1) as banks,
     ):
-        offsets = held.tile([FEATURES, ENTRIES // PER_COLUMN], U16, name="offsets")
+
+        offsets = held.tile([FEATURES, ENTRIES // PER_COLUMN], U16, name="offsets", align_bytes=DMA_BLOCK)
         nc.sync.dma_start(offsets[:], offs)
 
-        tokens = held.tile([FEATURES, TOKENS], BF16, name="tokens")
+        tokens = held.tile([FEATURES, TOKENS], BF16, name="tokens", align_bytes=DMA_BLOCK)
         nc.scalar.dma_start(tokens[:], table)
 
-        weights = held.tile([FEATURES, EXPERTS, HIDDEN], BF16, name="weights")
+        weights = held.tile([FEATURES, EXPERTS, HIDDEN], BF16, name="weights", align_bytes=DMA_BLOCK)
         nc.sync.dma_start(weights[:, 0:1, :], w[0:1].rearrange("e k m -> k e m"))
 
         bias = held.tile([HIDDEN, 1], F32, name="bias")
@@ -40,7 +42,7 @@ def tile_gather_matmul_kernel(tc, table, w, b, offs, out):
         warmed = held.tile([HIDDEN, 1], F32, name="warmed")
         nc.scalar.activation(warmed[:], zeros[:], GELU_TANH)
 
-        result = held.tile([HIDDEN, ENTRIES], F32, name="result")
+        result = held.tile([HIDDEN, ENTRIES], F32, name="result", align_bytes=DMA_BLOCK)
 
         for e in range(EXPERTS):
             columns = slice(e * PIECE, (e + 1) * PIECE)

@@ -34,8 +34,9 @@ def tile_gather_matmul_kernel(tc, table, w, b, offs, out):
         bias = held.tile([HIDDEN, 1], F32, name="bias")
         nc.sync.dma_start(bias[:], b)
 
-        for group in (slice(1, 2), slice(2, 4), slice(4, 6), slice(6, 8)):
-            nc.scalar.dma_start(weights[:, group, :], w[group].rearrange("e k m -> k e m"))
+        nc.scalar.dma_start(weights[:, 1:2, :], w[1:2].rearrange("e k m -> k e m"))
+        for group in (slice(2, 4), slice(4, 6), slice(6, 8)):
+            nc.sync.dma_start(weights[:, group, :], w[group].rearrange("e k m -> k e m"))
 
         zeros = held.tile([HIDDEN, 1], F32, name="zeros")
         nc.vector.memset(zeros[:], 0.0)

import concourse.mybir as mybir

BF16, F32, U16 = mybir.dt.bfloat16, mybir.dt.float32, mybir.dt.uint16
GELU_TANH = mybir.ActivationFunctionType.Gelu_apprx_tanh

FEATURES = 128
HIDDEN = 128
TOKENS = 1024
EXPERTS = 8
PIECE = 256
ENTRIES = EXPERTS * PIECE
PER_COLUMN = 16
DMA_BLOCK = 256

FLOPS = 2 * FEATURES * HIDDEN * ENTRIES


def tile_gather_matmul_kernel(tc, table, w, b, offs, out):
    nc = tc.nc
    with (
        tc.tile_pool(name="held", bufs=1) as held,
        tc.psum_pool(name="banks", bufs=1) as banks,
    ):

        offsets = held.tile([FEATURES, ENTRIES // PER_COLUMN], U16, name="offsets", align_bytes=DMA_BLOCK)
        nc.sync.dma_start(offsets[:], offs)

        tokens = held.tile([FEATURES, TOKENS], BF16, name="tokens", align_bytes=DMA_BLOCK)
        nc.scalar.dma_start(tokens[:], table)

        weights = held.tile([FEATURES, EXPERTS, HIDDEN], BF16, name="weights", align_bytes=DMA_BLOCK)
        nc.sync.dma_start(weights[:, 0:1, :], w[0:1].rearrange("e k m -> k e m"))

        bias = held.tile([HIDDEN, 1], F32, name="bias")
        nc.sync.dma_start(bias[:], b)

        nc.scalar.dma_start(weights[:, 1:2, :], w[1:2].rearrange("e k m -> k e m"))
        for group in (slice(2, 4), slice(4, 6), slice(6, 8)):
            nc.sync.dma_start(weights[:, group, :], w[group].rearrange("e k m -> k e m"))

        zeros = held.tile([HIDDEN, 1], F32, name="zeros")
        nc.vector.memset(zeros[:], 0.0)
        warmed = held.tile([HIDDEN, 1], F32, name="warmed")
        nc.scalar.activation(warmed[:], zeros[:], GELU_TANH)

        result = held.tile([HIDDEN, ENTRIES], F32, name="result", align_bytes=DMA_BLOCK)

        for e in range(EXPERTS):
            columns = slice(e * PIECE, (e + 1) * PIECE)
            piece = offsets[:, e * PIECE // PER_COLUMN : (e + 1) * PIECE // PER_COLUMN]

            bank = banks.tile([HIDDEN, PIECE], F32, name="bank%d" % e)
            nc.tensor.matmul(bank[:], weights[:, e, :], tokens[:].indirect(piece), start=True, stop=True)
            nc.scalar.activation(result[:, columns], bank[:], GELU_TANH, bias=bias[:, 0:1])
            nc.sync.dma_start(out[:, columns], result[:, columns])
